import numpy as np
import ml_dtypes


def mxq(x, axis, fmt="e4m3"):
    dtype, down = {"e4m3": (ml_dtypes.float8_e4m3fn, 7), "e5m2": (ml_dtypes.float8_e5m2, 14)}[fmt]
    v = np.moveaxis(np.asarray(x, np.float32).astype(ml_dtypes.bfloat16).astype(np.float64), axis, -1)
    blocks = v.reshape(v.shape[:-1] + (-1, 32))
    amax = np.abs(blocks).max(-1, keepdims=True)
    byte = np.maximum(np.where(amax > 0, np.frexp(amax)[1] - 1 + 127, 0) - down, 1)
    scale = np.exp2(byte - 127.0)
    codes = (blocks / scale).astype(np.float32).astype(dtype).astype(np.float64)
    return np.moveaxis((codes * scale).reshape(v.shape), -1, axis)


WIDE = False


def mx_kscale(k):
    if not WIDE:
        return np.ones(k)
    levels = np.array([10, -10, 5, -5, 0])
    if k % 512:
        return np.exp2(np.random.permutation(np.resize(levels, k // 32))).repeat(32)
    a = np.empty((k // 512, 16))
    for p in range(k // 512):
        a[p, :8] = np.random.permutation(np.resize(levels, 8))
        for g in range(8):
            far = levels[np.abs(levels - a[p, g]) >= 10]
            a[p, g + 8] = far[np.random.randint(len(far))]
    return np.exp2(a.ravel()).repeat(32)


def f64(x):
    return np.asarray(x).astype(np.float64)


def striped(idx):
    return np.tile(idx.reshape(-1, 16).T, (8, 1)).astype(np.uint16)


def unstriped(offs):
    return offs[:16].T.reshape(-1).astype(np.int64)


def striped8(idx):
    return np.concatenate([x.reshape(-1, 16).T for x in idx]).astype(np.uint16)


def runs(offs, k):
    lists = np.stack([offs[16 * r : 16 * r + 16].T.reshape(-1) for r in range(8)]).astype(np.int64)
    return lists[np.arange(k) % 512 // 64]


def pack_weight(w):
    k, n = w.shape
    w = f64(np.asarray(w, np.float32).astype(ml_dtypes.bfloat16)).reshape(k // 32, 32, n)
    amax = np.abs(w).max(1)
    byte = np.clip(np.where(amax > 0, np.frexp(amax)[1] - 1 + 127 - 7, 1), 1, 254)
    scaled = (w * np.exp2(127.0 - byte)[:, None, :]).reshape(k, n).astype(np.float32)
    words = np.ascontiguousarray(scaled.reshape(k // 512, 128, 4, n).transpose(0, 1, 3, 2)).astype(ml_dtypes.float8_e4m3fn).view(np.uint8)
    return words, np.ascontiguousarray(byte.astype(np.uint8).reshape(k // 512, 16, n))


def unpack_weight(words, scales):
    g, p, n, _ = words.shape
    vals = np.ascontiguousarray(words).view(ml_dtypes.float8_e4m3fn).astype(np.float64) * np.repeat(np.exp2(scales.astype(np.float64) - 127.0), 8, axis=1)[..., None]
    return vals.transpose(0, 1, 3, 2).reshape(g * 512, n)


def sigmoid(v):
    return 1.0 / (1.0 + np.exp(-np.maximum(v, -700.0)))

def planes(y):
    n, m = y.shape
    v = y.astype(np.float32).astype(ml_dtypes.bfloat16).astype(np.float64).reshape(n // 32, 32, m)
    top = np.abs(v).max(1)
    byte = np.clip(np.where(top > 0, np.frexp(top)[1] - 1 + 127 - 7, 1), 1, 254)
    codes = (v * np.exp2(127.0 - byte)[:, None, :]).reshape(n, m).astype(np.float32).astype(ml_dtypes.float8_e4m3fn).view(np.uint8)
    words = codes.reshape(n // 512, 128, 4, m).transpose(0, 1, 3, 2)
    return np.ascontiguousarray(words), np.ascontiguousarray(byte.astype(np.uint8).reshape(n // 512, 16, m))


K, T, S, V, G, H = 512, 2048, 1024, 512, 2048, 512


def setup_inputs():
    n = np.random.standard_normal
    s = mx_kscale(K)[:, None]
    packed_xT = pack_weight(n((K, T)) * s)
    packed_dT = pack_weight(n((K, G)) / s)
    return {
        "x_words": packed_xT[0],
        "x_scales": packed_xT[1],
        "d_words": packed_dT[0],
        "d_scales": packed_dT[1],
        "gs": (np.random.uniform(0.5, 1.5, (K, 1)) * s).astype(np.float32),
        "offs": striped(np.random.permutation(T)[:S]),
        "k1": striped8(np.random.randint(0, G, (8, H))),
        "n1": striped8(np.stack([np.random.permutation(S) for _ in range(8)])),
        "k2": striped8(np.random.randint(0, G, (8, H))),
        "n2": striped8(np.stack([np.random.permutation(V) for _ in range(8)])),
        "n3": striped8(np.stack([np.random.permutation(V) for _ in range(8)])),
        "n4": striped8(np.stack([np.random.permutation(V) for _ in range(8)])),
    }


def reference(x_words, x_scales, d_words, d_scales, gs, offs, k1, n1, k2, n2, n3, n4):
    d_k2 = unpack_weight(d_words, d_scales)[np.arange(K)[:, None], runs(k2, K)]
    d_k1 = unpack_weight(d_words, d_scales)[np.arange(K)[:, None], runs(k1, K)]
    xq = unpack_weight(x_words, x_scales)[:, unstriped(offs)]
    h = 0.0625 * (d_k1.T @ xq)
    ln = h[np.arange(H)[:, None], runs(n1, H)]
    z = f64(gs) * (ln.reshape(H, V, 2).max(axis=2))
    h2 = 0.0625 * ((d_k2.T @ mxq(z, 0, "e4m3")))
    pa = h2[np.arange(H)[:, None], runs(n2, H)]
    out_0 = pa + (sigmoid(h2[np.arange(H)[:, None], runs(n3, H)])) * (h2[np.arange(H)[:, None], runs(n4, H)] - pa)
    return (out_0,) + planes(out_0)

@@ -1,0 +1,184 @@
+from contextlib import ExitStack
+
+import concourse.mybir as mybir
+
+F32 = mybir.dt.float32
+BF16 = mybir.dt.bfloat16
+I32 = mybir.dt.int32
+U32 = mybir.dt.uint32
+U16 = mybir.dt.uint16
+U8 = mybir.dt.uint8
+FP8X4 = mybir.dt.float8_e4m3fn_x4
+ALU = mybir.AluOpType
+ACT = mybir.ActivationFunctionType
+
+P = 128
+PACK = 4
+K, T, S, V, G, H = 512, 2048, 1024, 512, 2048, 512
+BANK = 512
+SIXTEENTH = 0.0625
+FLOPS = 2 * K * H * S + 2 * K * H * V
+
+Z_CHUNKS = ((0, 256), (256, 384), (384, 512))
+OUT_CHUNKS = ((0, 256), (256, 512))
+
+
+def entries(lists, first, last):
+    return lists[:, first // 16 : last // 16]
+
+
+def tile_picked_codepoollerp_none_po_kernel(tc, x_words, x_scales, d_words, d_scales, gs, offs, k1, n1, k2, n2, n3, n4, out_0, out_1, out_2):
+    nc = tc.nc
+    with ExitStack() as ctx:
+        keep = ctx.enter_context(tc.tile_pool(name="keep", bufs=1))
+        psum = ctx.enter_context(tc.psum_pool(name="psum", bufs=8))
+
+        def load_list(name, src):
+            lists = keep.tile(list(src.shape), U16, name=name)
+            nc.sync.dma_start(lists[:], src)
+            return lists
+
+        def load_words(name, src):
+            table = keep.tile([P, src.shape[2]], I32, name=name, align_bytes=64)
+            nc.sync.dma_start(table[:], src[0].rearrange("p c r -> p (c r)").bitcast(I32))
+            return table
+
+        d_byte_table = keep.tile([P, G], U8, align_bytes=64)
+        x_byte_table = keep.tile([P, T], U8, align_bytes=64)
+        nc.vector.memset(d_byte_table[:].bitcast(I32), 0)
+        nc.vector.memset(x_byte_table[:].bitcast(I32), 0)
+
+        k1_l = load_list("k1_l", k1)
+        for e in range(2):
+            nc.scalar.dma_start(d_byte_table[:].bitcast(I32)[e:P:16, :], d_scales[0].bitcast(I32)[e:16:2, :])
+        offs_l = load_list("offs_l", offs)
+        for q in range(4):
+            nc.scalar.dma_start(x_byte_table[:].bitcast(I32)[32 * q : 32 * q + 4, :], x_scales[0].bitcast(I32)[4 * q : 4 * q + 4, :])
+        d_word_table = load_words("d_word_table", d_words)
+        x_word_table = load_words("x_word_table", x_words)
+        k2_l = load_list("k2_l", k2)
+        n1_l = load_list("n1_l", n1)
+        gain = keep.tile([P, PACK], F32)
+        nc.sync.dma_start(gain[:], gs.rearrange("(p t) o -> p (t o)", t=PACK))
+        n3_l = load_list("n3_l", n3)
+        n2_l = load_list("n2_l", n2)
+        n4_l = load_list("n4_l", n4)
+
+        def pick_bytes(name, lists):
+            picked = keep.tile([P, H], U8, name=name + "_picked", align_bytes=64)
+            nc.vector.tensor_copy(picked[:], d_byte_table[:].indirect(lists[:]))
+            dealt = keep.tile([P, H], U8, name=name + "_dealt", align_bytes=64)
+            nc.vector.tensor_copy(
+                dealt[:].rearrange("p (t c i) -> p c t i", t=PACK, i=16),
+                picked[:].rearrange("p (c i t) -> p c t i", t=PACK, i=16),
+            )
+            for e in range(2):
+                nc.sync.dma_start(dealt[:].bitcast(I32)[2 + e : P : 32, :], dealt[:].bitcast(I32)[16 + e : P : 32, :])
+            return dealt
+
+        def pick_words(name, lists):
+            picked = keep.tile([P, H], U32, name=name + "_picked", align_bytes=64)
+            nc.vector.tensor_copy(picked[:], d_word_table[:].bitcast(U32).indirect(lists[:]))
+            dealt = keep.tile([P, H], U32, name=name + "_dealt", align_bytes=64)
+            nc.vector.tensor_copy(
+                dealt[:].rearrange("p (t c i) -> p c t i", t=PACK, i=4),
+                picked[:].rearrange("p (c i t) -> p c t i", t=PACK, i=4),
+            )
+            return dealt
+
+        def multiply(out, words, scales, t, rhs_words, rhs_scales):
+            cols = slice(t * P, (t + 1) * P)
+            nc.tensor.matmul_mx(
+                out=out, lhsT=words[:, cols].bitcast(FP8X4), lhsT_scale=scales[:, cols],
+                rhs=rhs_words.bitcast(FP8X4), rhs_scale=rhs_scales, start=True, stop=True,
+            )
+
+        w1_scales = pick_bytes("w1_scales", k1_l)
+        halves = range(S // BANK)
+        x_bytes = [keep.tile([P, BANK], U8, name="x_bytes%d" % u, align_bytes=64) for u in halves]
+        x_codes = [keep.tile([P, BANK], U32, name="x_codes%d" % u, align_bytes=64) for u in halves]
+        for u in halves:
+            nc.vector.tensor_copy(x_bytes[u][:], x_byte_table[:].indirect(entries(offs_l, u * BANK, (u + 1) * BANK)))
+        w1_words = pick_words("w1_words", k1_l)
+        for u in halves:
+            nc.vector.tensor_copy(x_codes[u][:], x_word_table[:].bitcast(U32).indirect(entries(offs_l, u * BANK, (u + 1) * BANK)))
+
+        h = [keep.tile([P, S], F32, name="h%d" % t) for t in range(PACK)]
+        for t in range(PACK):
+            for u in halves:
+                acc = psum.tile([P, BANK], F32, name="acc")
+                multiply(acc[:], w1_words, w1_scales, t, x_codes[u][:], x_bytes[u][:])
+                nc.scalar.activation(h[t][:, u * BANK : (u + 1) * BANK], acc[:], ACT.Copy, scale=SIXTEENTH)
+
+        w2_scales = pick_bytes("w2_scales", k2_l)
+
+        z_bf = []
+        for c, (v0, v1) in enumerate(Z_CHUNKS):
+            n = v1 - v0
+            lined = keep.tile([P, PACK, 2 * n], F32, name="lined%d" % c)
+            larger = keep.tile([P, PACK, n], F32, name="larger%d" % c)
+            z_rows = keep.tile([P, PACK, n], BF16, name="z_rows%d" % c)
+            z_woven = keep.tile([P, n, PACK], BF16, name="z_woven%d" % c, align_bytes=64)
+            for t in range(PACK):
+                nc.vector.tensor_copy(lined[:, t, :], h[t][:].indirect(entries(n1_l, 2 * v0, 2 * v1)))
+            for t0 in (0, 2):
+                pairs = lined[:, t0 : t0 + 2, :].rearrange("p t (v e) -> p (t v) e", e=2)
+                nc.vector.tensor_tensor(larger[:, t0 : t0 + 2, :].rearrange("p t v -> p (t v)"), pairs[:, :, 0], pairs[:, :, 1], ALU.max)
+            for t in range(PACK):
+                nc.scalar.activation(z_rows[:, t, :], larger[:, t, :], ACT.Copy, scale=gain[:, t : t + 1])
+            nc.scalar.copy(
+                z_woven[:].rearrange("p (c i) t -> p c t i", i=4),
+                z_rows[:].rearrange("p t (c i) -> p c t i", i=4),
+            )
+            z_bf.append(z_woven)
+
+        w2_words = pick_words("w2_words", k2_l)
+
+        z_codes = keep.tile([P, V], U32, align_bytes=64)
+        z_bytes = keep.tile([P, V], U8, align_bytes=64)
+        for c, (v0, v1) in enumerate(Z_CHUNKS):
+            nc.vector.quantize_mx(
+                out=z_codes[:, v0:v1].bitcast(FP8X4), scales=z_bytes[:, v0:v1],
+                in_=z_bf[c][:].rearrange("p v t -> p (v t)"),
+            )
+
+        h2 = [keep.tile([P, V], F32, name="h2_%d" % t) for t in range(PACK)]
+        for t in range(PACK):
+            acc = psum.tile([P, BANK], F32, name="acc")
+            for v0, v1 in Z_CHUNKS:
+                multiply(acc[:, v0:v1], w2_words, w2_scales, t, z_codes[:, v0:v1], z_bytes[:, v0:v1])
+            nc.scalar.activation(h2[t][:], acc[:], ACT.Copy, scale=SIXTEENTH)
+
+        out_rows = out_0.rearrange("(p t) v -> p t v", t=PACK)
+        out_words = out_1[0].rearrange("p c r -> p (c r)").bitcast(I32)
+        out_bytes = keep.tile([P, V], U8, align_bytes=64)
+        for c, (v0, v1) in enumerate(OUT_CHUNKS):
+            n = v1 - v0
+            gate = keep.tile([P, PACK, n], F32, name="gate%d" % c)
+            rest = keep.tile([P, PACK, n], F32, name="rest%d" % c)
+            far = keep.tile([P, PACK, n], F32, name="far%d" % c)
+            near = keep.tile([P, PACK, n], F32, name="near%d" % c)
+            mixed = keep.tile([P, PACK, n], F32, name="mixed%d" % c)
+            woven = keep.tile([P, n, PACK], BF16, name="woven%d" % c, align_bytes=64)
+            codes = keep.tile([P, n], U32, name="codes%d" % c, align_bytes=64)
+            for t in range(PACK):
+                nc.scalar.activation(gate[:, t, :], h2[t][:].indirect(entries(n3_l, v0, v1)), ACT.Sigmoid)
+                nc.scalar.activation(rest[:, t, :], gate[:, t, :], ACT.Copy, scale=-1.0, bias=1.0)
+                nc.vector.tensor_tensor(far[:, t, :], h2[t][:].indirect(entries(n4_l, v0, v1)), gate[:, t, :], ALU.mult)
+                nc.vector.tensor_tensor(near[:, t, :], h2[t][:].indirect(entries(n2_l, v0, v1)), rest[:, t, :], ALU.mult)
+            for t0 in (0, 2):
+                nc.vector.tensor_tensor(mixed[:, t0 : t0 + 2, :], near[:, t0 : t0 + 2, :], far[:, t0 : t0 + 2, :], ALU.add)
+            nc.sync.dma_start(out_rows[:, :, v0:v1], mixed[:])
+            weave = nc.vector.tensor_copy if c == len(OUT_CHUNKS) - 1 else nc.scalar.copy
+            weave(
+                woven[:].rearrange("p (c i) t -> p c t i", i=4),
+                mixed[:].rearrange("p t (c i) -> p c t i", i=4),
+            )
+            nc.vector.quantize_mx(
+                out=codes[:].bitcast(FP8X4), scales=out_bytes[:, v0:v1],
+                in_=woven[:].rearrange("p v t -> p (v t)"),
+            )
+            nc.sync.dma_start(out_words[:, v0:v1], codes[:].bitcast(I32))
+        for q in range(4):
+            queue = nc.scalar if q % 2 else nc.sync
+            queue.dma_start(out_2[0].bitcast(I32)[4 * q : 4 * q + 4, :], out_bytes[:].bitcast(I32)[32 * q : 32 * q + 4, :])

@@ -38,9 +38,9 @@ def tile_picked_codepoollerp_none_po_kernel(tc, x_words, x_scales, d_words, d_sc
             nc.sync.dma_start(lists[:], src)
             return lists
 
-        def load_words(name, src):
-            table = keep.tile([P, src.shape[2]], I32, name=name, align_bytes=64)
-            nc.sync.dma_start(table[:], src[0].rearrange("p c r -> p (c r)").bitcast(I32))
+        def load_words(name, src, queue):
+            table = keep.tile([P, src.shape[2]], I32, name=name, tag=name, align_bytes=64)
+            queue.dma_start(table[:], src[0].rearrange("p c r -> p (c r)").bitcast(I32))
             return table
 
         d_byte_table = keep.tile([P, G], U8, align_bytes=64)
@@ -48,36 +48,39 @@ def tile_picked_codepoollerp_none_po_kernel(tc, x_words, x_scales, d_words, d_sc
         nc.vector.memset(d_byte_table[:].bitcast(I32), 0)
         nc.vector.memset(x_byte_table[:].bitcast(I32), 0)
 
+        d_word_table = load_words("d_word_table", d_words, nc.scalar)
         k1_l = load_list("k1_l", k1)
-        for e in range(2):
-            nc.scalar.dma_start(d_byte_table[:].bitcast(I32)[e:P:16, :], d_scales[0].bitcast(I32)[e:16:2, :])
         offs_l = load_list("offs_l", offs)
-        for q in range(4):
-            nc.scalar.dma_start(x_byte_table[:].bitcast(I32)[32 * q : 32 * q + 4, :], x_scales[0].bitcast(I32)[4 * q : 4 * q + 4, :])
-        d_word_table = load_words("d_word_table", d_words)
-        x_word_table = load_words("x_word_table", x_words)
         k2_l = load_list("k2_l", k2)
         n1_l = load_list("n1_l", n1)
+        n3_l = load_list("n3_l", n3)
+        n4_l = load_list("n4_l", n4)
+        n2_l = load_list("n2_l", n2)
         gain = keep.tile([P, PACK], F32)
         nc.sync.dma_start(gain[:], gs.rearrange("(p t) o -> p (t o)", t=PACK))
-        n3_l = load_list("n3_l", n3)
-        n2_l = load_list("n2_l", n2)
-        n4_l = load_list("n4_l", n4)
+        x_word_table = load_words("x_word_table", x_words, nc.sync)
+        nc.scalar.dma_start(d_byte_table[:].bitcast(I32)[0:P:8, :], d_scales[0].bitcast(I32))
+        for q in range(4):
+            nc.scalar.dma_start(x_byte_table[:].bitcast(I32)[32 * q : 32 * q + 4, :], x_scales[0].bitcast(I32)[4 * q : 4 * q + 4, :])
+        warm = keep.tile([P, 1], F32)
+        nc.scalar.activation(warm[:], gain[:, 0:1], ACT.Sigmoid)
 
-        def pick_bytes(name, lists):
-            picked = keep.tile([P, H], U8, name=name + "_picked", align_bytes=64)
+        def pick_bytes(name, lists, tag):
+            picked = keep.tile([P, H], U8, name=name + "_picked", tag=tag, align_bytes=64)
             nc.vector.tensor_copy(picked[:], d_byte_table[:].indirect(lists[:]))
             dealt = keep.tile([P, H], U8, name=name + "_dealt", align_bytes=64)
             nc.vector.tensor_copy(
                 dealt[:].rearrange("p (t c i) -> p c t i", t=PACK, i=16),
                 picked[:].rearrange("p (c i t) -> p c t i", t=PACK, i=16),
             )
-            for e in range(2):
-                nc.sync.dma_start(dealt[:].bitcast(I32)[2 + e : P : 32, :], dealt[:].bitcast(I32)[16 + e : P : 32, :])
-            return dealt
+            placed = keep.tile([P, H], U8, name=name + "_placed", align_bytes=64)
+            nc.gpsimd.memset(placed[:].bitcast(I32), 0)
+            for q in range(4):
+                nc.sync.dma_start(placed[:].bitcast(I32)[32 * q : 32 * q + 4, :], dealt[:].bitcast(I32)[32 * q : 32 * q + 32 : 8, :])
+            return placed
 
-        def pick_words(name, lists):
-            picked = keep.tile([P, H], U32, name=name + "_picked", align_bytes=64)
+        def pick_words(name, lists, tag):
+            picked = keep.tile([P, H], U32, name=name + "_picked", tag=tag, align_bytes=64)
             nc.vector.tensor_copy(picked[:], d_word_table[:].bitcast(U32).indirect(lists[:]))
             dealt = keep.tile([P, H], U32, name=name + "_dealt", align_bytes=64)
             nc.vector.tensor_copy(
@@ -93,37 +96,36 @@ def tile_picked_codepoollerp_none_po_kernel(tc, x_words, x_scales, d_words, d_sc
                 rhs=rhs_words.bitcast(FP8X4), rhs_scale=rhs_scales, start=True, stop=True,
             )
 
-        w1_scales = pick_bytes("w1_scales", k1_l)
-        halves = range(S // BANK)
-        x_bytes = [keep.tile([P, BANK], U8, name="x_bytes%d" % u, align_bytes=64) for u in halves]
-        x_codes = [keep.tile([P, BANK], U32, name="x_codes%d" % u, align_bytes=64) for u in halves]
-        for u in halves:
-            nc.vector.tensor_copy(x_bytes[u][:], x_byte_table[:].indirect(entries(offs_l, u * BANK, (u + 1) * BANK)))
-        w1_words = pick_words("w1_words", k1_l)
-        for u in halves:
-            nc.vector.tensor_copy(x_codes[u][:], x_word_table[:].bitcast(U32).indirect(entries(offs_l, u * BANK, (u + 1) * BANK)))
-
+        w1_words = pick_words("w1_words", k1_l, "w1_words_picked")
+        w1_scales = pick_bytes("w1_scales", k1_l, "w1_scales_picked")
         h = [keep.tile([P, S], F32, name="h%d" % t) for t in range(PACK)]
-        for t in range(PACK):
-            for u in halves:
+        for u in range(S // BANK):
+            x_bytes = keep.tile([P, BANK], U8, name="x_bytes%d" % u, align_bytes=64)
+            x_codes = keep.tile([P, BANK], U32, name="x_codes%d" % u, align_bytes=64)
+            tokens = entries(offs_l, u * BANK, (u + 1) * BANK)
+            nc.vector.tensor_copy(x_bytes[:], x_byte_table[:].indirect(tokens))
+            nc.vector.tensor_copy(x_codes[:], x_word_table[:].bitcast(U32).indirect(tokens))
+            for t in range(PACK):
                 acc = psum.tile([P, BANK], F32, name="acc")
-                multiply(acc[:], w1_words, w1_scales, t, x_codes[u][:], x_bytes[u][:])
+                multiply(acc[:], w1_words, w1_scales, t, x_codes[:], x_bytes[:])
                 nc.scalar.activation(h[t][:, u * BANK : (u + 1) * BANK], acc[:], ACT.Copy, scale=SIXTEENTH)
 
-        w2_scales = pick_bytes("w2_scales", k2_l)
+        w2_scales = pick_bytes("w2_scales", k2_l, "x_word_table")
 
         z_bf = []
         for c, (v0, v1) in enumerate(Z_CHUNKS):
             n = v1 - v0
-            lined = keep.tile([P, PACK, 2 * n], F32, name="lined%d" % c)
-            larger = keep.tile([P, PACK, n], F32, name="larger%d" % c)
+            lined_a = keep.tile([P, PACK - 1, 2 * n], F32, name="lined_a%d" % c, tag="lined_a")
+            lined_b = keep.tile([P, 1, 2 * n], F32, name="lined_b%d" % c, tag="lined_b")
+            larger = keep.tile([P, PACK, n], F32, name="larger%d" % c, tag="larger%d" % c, align_bytes=64)
             z_rows = keep.tile([P, PACK, n], BF16, name="z_rows%d" % c)
             z_woven = keep.tile([P, n, PACK], BF16, name="z_woven%d" % c, align_bytes=64)
             for t in range(PACK):
-                nc.vector.tensor_copy(lined[:, t, :], h[t][:].indirect(entries(n1_l, 2 * v0, 2 * v1)))
-            for t0 in (0, 2):
-                pairs = lined[:, t0 : t0 + 2, :].rearrange("p t (v e) -> p (t v) e", e=2)
-                nc.vector.tensor_tensor(larger[:, t0 : t0 + 2, :].rearrange("p t v -> p (t v)"), pairs[:, :, 0], pairs[:, :, 1], ALU.max)
+                dst = lined_a[:, t, :] if t < PACK - 1 else lined_b[:, 0, :]
+                nc.vector.tensor_copy(dst, h[t][:].indirect(entries(n1_l, 2 * v0, 2 * v1)))
+            for part, rows in ((lined_a, slice(0, PACK - 1)), (lined_b, slice(PACK - 1, PACK))):
+                pairs = part[:].rearrange("p t (v e) -> p (t v) e", e=2)
+                nc.vector.tensor_tensor(larger[:, rows, :].rearrange("p t v -> p (t v)"), pairs[:, :, 0], pairs[:, :, 1], ALU.max)
             for t in range(PACK):
                 nc.scalar.activation(z_rows[:, t, :], larger[:, t, :], ACT.Copy, scale=gain[:, t : t + 1])
             nc.scalar.copy(
@@ -132,7 +134,7 @@ def tile_picked_codepoollerp_none_po_kernel(tc, x_words, x_scales, d_words, d_sc
             )
             z_bf.append(z_woven)
 
-        w2_words = pick_words("w2_words", k2_l)
+        w2_words = pick_words("w2_words", k2_l, "larger1")
 
         z_codes = keep.tile([P, V], U32, align_bytes=64)
         z_bytes = keep.tile([P, V], U8, align_bytes=64)
@@ -143,42 +145,82 @@ def tile_picked_codepoollerp_none_po_kernel(tc, x_words, x_scales, d_words, d_sc
             )
 
         h2 = [keep.tile([P, V], F32, name="h2_%d" % t) for t in range(PACK)]
-        for t in range(PACK):
-            acc = psum.tile([P, BANK], F32, name="acc")
-            for v0, v1 in Z_CHUNKS:
-                multiply(acc[:, v0:v1], w2_words, w2_scales, t, z_codes[:, v0:v1], z_bytes[:, v0:v1])
-            nc.scalar.activation(h2[t][:], acc[:], ACT.Copy, scale=SIXTEENTH)
+
+        def second_layer(t):
+            for group in (Z_CHUNKS[:-1], Z_CHUNKS[-1:]):
+                acc = psum.tile([P, BANK], F32, name="acc")
+                for v0, v1 in group:
+                    multiply(acc[:, v0:v1], w2_words, w2_scales, t, z_codes[:, v0:v1], z_bytes[:, v0:v1])
+                cols = slice(group[0][0], group[-1][1])
+                nc.scalar.activation(h2[t][:, cols], acc[:, cols], ACT.Copy, scale=SIXTEENTH)
 
         out_rows = out_0.rearrange("(p t) v -> p t v", t=PACK)
         out_words = out_1[0].rearrange("p c r -> p (c r)").bitcast(I32)
         out_bytes = keep.tile([P, V], U8, align_bytes=64)
-        for c, (v0, v1) in enumerate(OUT_CHUNKS):
-            n = v1 - v0
-            gate = keep.tile([P, PACK, n], F32, name="gate%d" % c)
-            rest = keep.tile([P, PACK, n], F32, name="rest%d" % c)
-            far = keep.tile([P, PACK, n], F32, name="far%d" % c)
-            near = keep.tile([P, PACK, n], F32, name="near%d" % c)
-            mixed = keep.tile([P, PACK, n], F32, name="mixed%d" % c)
-            woven = keep.tile([P, n, PACK], BF16, name="woven%d" % c, align_bytes=64)
-            codes = keep.tile([P, n], U32, name="codes%d" % c, align_bytes=64)
-            for t in range(PACK):
-                nc.scalar.activation(gate[:, t, :], h2[t][:].indirect(entries(n3_l, v0, v1)), ACT.Sigmoid)
-                nc.scalar.activation(rest[:, t, :], gate[:, t, :], ACT.Copy, scale=-1.0, bias=1.0)
-                nc.vector.tensor_tensor(far[:, t, :], h2[t][:].indirect(entries(n4_l, v0, v1)), gate[:, t, :], ALU.mult)
-                nc.vector.tensor_tensor(near[:, t, :], h2[t][:].indirect(entries(n2_l, v0, v1)), rest[:, t, :], ALU.mult)
-            for t0 in (0, 2):
-                nc.vector.tensor_tensor(mixed[:, t0 : t0 + 2, :], near[:, t0 : t0 + 2, :], far[:, t0 : t0 + 2, :], ALU.add)
-            nc.sync.dma_start(out_rows[:, :, v0:v1], mixed[:])
-            weave = nc.vector.tensor_copy if c == len(OUT_CHUNKS) - 1 else nc.scalar.copy
-            weave(
-                woven[:].rearrange("p (c i) t -> p c t i", i=4),
-                mixed[:].rearrange("p t (c i) -> p c t i", i=4),
+        def chunk_tiles(name, dtype):
+            return [keep.tile([P, PACK, v1 - v0], dtype, name="%s%d" % (name, c), align_bytes=64) for c, (v0, v1) in enumerate(OUT_CHUNKS)]
+
+        gate, rest, far, near, mixed = (chunk_tiles(name, F32) for name in ("gate", "rest", "far", "near", "mixed"))
+        woven = chunk_tiles("woven", BF16)
+
+        def fetch(c, t):
+            v0, v1 = OUT_CHUNKS[c]
+            nc.scalar.activation(gate[c][:, t, :], h2[t][:].indirect(entries(n3_l, v0, v1)), ACT.Sigmoid)
+            nc.scalar.activation(rest[c][:, t, :], gate[c][:, t, :], ACT.Copy, scale=-1.0, bias=1.0)
+            nc.vector.tensor_tensor(far[c][:, t, :], h2[t][:].indirect(entries(n4_l, v0, v1)), gate[c][:, t, :], ALU.mult)
+            nc.vector.tensor_tensor(near[c][:, t, :], h2[t][:].indirect(entries(n2_l, v0, v1)), rest[c][:, t, :], ALU.mult)
+
+        def fetch_first(c, t):
+            v0, v1 = OUT_CHUNKS[c]
+            step = keep.tile([P, v1 - v0], F32)
+            nc.scalar.activation(gate[c][:, t, :], h2[t][:].indirect(entries(n3_l, v0, v1)), ACT.Sigmoid)
+            nc.vector.tensor_copy(near[c][:, t, :], h2[t][:].indirect(entries(n2_l, v0, v1)))
+            nc.vector.tensor_tensor(step[:], h2[t][:].indirect(entries(n4_l, v0, v1)), near[c][:, t, :], ALU.subtract)
+            nc.vector.tensor_tensor(far[c][:, t, :], step[:], gate[c][:, t, :], ALU.mult)
+
+        def mix(c, t0, count=2):
+            v0, v1 = OUT_CHUNKS[c]
+            rows = slice(t0, t0 + count)
+            nc.vector.tensor_tensor(mixed[c][:, rows, :], near[c][:, rows, :], far[c][:, rows, :], ALU.add)
+            nc.sync.dma_start(out_rows[:, rows, v0:v1], mixed[c][:, rows, :])
+
+        def weave(c, copy, quads):
+            copy(
+                woven[c][:].rearrange("p t v -> p (t v)").rearrange("p (c i t) -> p c t i", i=4, t=PACK)[:, quads],
+                mixed[c][:].rearrange("p t (c i) -> p c t i", i=4)[:, quads],
             )
+
+        def hand_on(c):
+            v0, v1 = OUT_CHUNKS[c]
+            codes = keep.tile([P, v1 - v0], U32, name="codes%d" % c, align_bytes=64)
             nc.vector.quantize_mx(
                 out=codes[:].bitcast(FP8X4), scales=out_bytes[:, v0:v1],
-                in_=woven[:].rearrange("p v t -> p (v t)"),
+                in_=woven[c][:].rearrange("p t v -> p (t v)"),
             )
             nc.sync.dma_start(out_words[:, v0:v1], codes[:].bitcast(I32))
+
+        second_layer(0)
+        fetch_first(0, 0)
+        second_layer(1)
+        fetch(1, 0)
+        fetch(0, 1)
+        second_layer(2)
+        fetch(1, 1)
+        mix(0, 0)
+        fetch(0, 2)
+        second_layer(3)
+        mix(1, 0)
+        fetch(0, 3)
+        fetch(1, 2)
+        mix(0, 2)
+        mix(1, 2, 1)
+        fetch(1, 3)
+        weave(0, nc.scalar.copy, slice(0, 64))
+        mix(1, 3, 1)
+        hand_on(0)
+        weave(1, nc.scalar.copy, slice(0, 24))
+        weave(1, nc.vector.tensor_copy, slice(24, 64))
+        hand_on(1)
         for q in range(4):
             queue = nc.scalar if q % 2 else nc.sync
             queue.dma_start(out_2[0].bitcast(I32)[4 * q : 4 * q + 4, :], out_bytes[:].bitcast(I32)[32 * q : 32 * q + 4, :])

@@ -19,8 +19,7 @@ BANK = 512
 SIXTEENTH = 0.0625
 FLOPS = 2 * K * H * S + 2 * K * H * V
 
-Z_CHUNKS = ((0, 256), (256, 384), (384, 512))
-OUT_CHUNKS = ((0, 256), (256, 512))
+Z_CHUNKS = ((0, 256), (256, 512))
 
 
 def entries(lists, first, last):
@@ -48,7 +47,10 @@ def tile_picked_codepoollerp_none_po_kernel(tc, x_words, x_scales, d_words, d_sc
         nc.vector.memset(d_byte_table[:].bitcast(I32), 0)
         nc.vector.memset(x_byte_table[:].bitcast(I32), 0)
 
-        d_word_table = load_words("d_word_table", d_words, nc.scalar)
+        warm = keep.tile([P, 1], F32, tag="x_word_table", align_bytes=64)
+        nc.gpsimd.memset(warm[:], 0.0)
+        nc.scalar.activation(warm[:], warm[:], ACT.Sigmoid)
+        d_word_table = load_words("d_word_table", d_words, nc.sync)
         k1_l = load_list("k1_l", k1)
         offs_l = load_list("offs_l", offs)
         k2_l = load_list("k2_l", k2)
@@ -57,37 +59,31 @@ def tile_picked_codepoollerp_none_po_kernel(tc, x_words, x_scales, d_words, d_sc
         n4_l = load_list("n4_l", n4)
         n2_l = load_list("n2_l", n2)
         gain = keep.tile([P, PACK], F32)
-        nc.sync.dma_start(gain[:], gs.rearrange("(p t) o -> p (t o)", t=PACK))
-        x_word_table = load_words("x_word_table", x_words, nc.sync)
+        nc.scalar.dma_start(gain[:], gs.rearrange("(p t) o -> p (t o)", t=PACK))
         nc.scalar.dma_start(d_byte_table[:].bitcast(I32)[0:P:8, :], d_scales[0].bitcast(I32))
         for q in range(4):
             nc.scalar.dma_start(x_byte_table[:].bitcast(I32)[32 * q : 32 * q + 4, :], x_scales[0].bitcast(I32)[4 * q : 4 * q + 4, :])
-        warm = keep.tile([P, 1], F32)
-        nc.scalar.activation(warm[:], gain[:, 0:1], ACT.Sigmoid)
+        x_word_table = load_words("x_word_table", x_words, nc.scalar)
 
-        def pick_bytes(name, lists, tag):
-            picked = keep.tile([P, H], U8, name=name + "_picked", tag=tag, align_bytes=64)
-            nc.vector.tensor_copy(picked[:], d_byte_table[:].indirect(lists[:]))
-            dealt = keep.tile([P, H], U8, name=name + "_dealt", align_bytes=64)
+        def pick(name, table, dtype, lists, tag):
+            picked = keep.tile([P, H], dtype, name=name, tag=tag, align_bytes=64)
+            nc.vector.tensor_copy(picked[:], table.indirect(lists[:]))
+            return picked
+
+        def deal(name, picked, dtype, run):
+            dealt = keep.tile([P, H], dtype, name=name, align_bytes=64)
             nc.vector.tensor_copy(
-                dealt[:].rearrange("p (t c i) -> p c t i", t=PACK, i=16),
-                picked[:].rearrange("p (c i t) -> p c t i", t=PACK, i=16),
+                dealt[:].rearrange("p (t c i) -> p c t i", t=PACK, i=run),
+                picked[:].rearrange("p (c i t) -> p c t i", t=PACK, i=run),
             )
-            placed = keep.tile([P, H], U8, name=name + "_placed", align_bytes=64)
+            return dealt
+
+        def place(name, dealt):
+            placed = keep.tile([P, H], U8, name=name, align_bytes=64)
             nc.gpsimd.memset(placed[:].bitcast(I32), 0)
             for q in range(4):
                 nc.sync.dma_start(placed[:].bitcast(I32)[32 * q : 32 * q + 4, :], dealt[:].bitcast(I32)[32 * q : 32 * q + 32 : 8, :])
             return placed
-
-        def pick_words(name, lists, tag):
-            picked = keep.tile([P, H], U32, name=name + "_picked", tag=tag, align_bytes=64)
-            nc.vector.tensor_copy(picked[:], d_word_table[:].bitcast(U32).indirect(lists[:]))
-            dealt = keep.tile([P, H], U32, name=name + "_dealt", align_bytes=64)
-            nc.vector.tensor_copy(
-                dealt[:].rearrange("p (t c i) -> p c t i", t=PACK, i=4),
-                picked[:].rearrange("p (c i t) -> p c t i", t=PACK, i=4),
-            )
-            return dealt
 
         def multiply(out, words, scales, t, rhs_words, rhs_scales):
             cols = slice(t * P, (t + 1) * P)
@@ -96,36 +92,41 @@ def tile_picked_codepoollerp_none_po_kernel(tc, x_words, x_scales, d_words, d_sc
                 rhs=rhs_words.bitcast(FP8X4), rhs_scale=rhs_scales, start=True, stop=True,
             )
 
-        w1_words = pick_words("w1_words", k1_l, "w1_words_picked")
-        w1_scales = pick_bytes("w1_scales", k1_l, "w1_scales_picked")
+        w1_words_picked = pick("w1_words_picked", d_word_table[:].bitcast(U32), U32, k1_l, "w1_words_picked")
+        w1_bytes_picked = pick("w1_bytes_picked", d_byte_table[:], U8, k1_l, "w1_bytes_picked")
+        w1_words = deal("w1_words", w1_words_picked, U32, 4)
+        w1_scales = place("w1_scales", deal("w1_bytes", w1_bytes_picked, U8, 16))
         h = [keep.tile([P, S], F32, name="h%d" % t) for t in range(PACK)]
-        for u in range(S // BANK):
-            x_bytes = keep.tile([P, BANK], U8, name="x_bytes%d" % u, align_bytes=64)
-            x_codes = keep.tile([P, BANK], U32, name="x_codes%d" % u, align_bytes=64)
-            tokens = entries(offs_l, u * BANK, (u + 1) * BANK)
-            nc.vector.tensor_copy(x_bytes[:], x_byte_table[:].indirect(tokens))
-            nc.vector.tensor_copy(x_codes[:], x_word_table[:].bitcast(U32).indirect(tokens))
-            for t in range(PACK):
+        halves = range(S // BANK)
+        x_bytes = [keep.tile([P, BANK], U8, name="x_bytes%d" % u, align_bytes=64) for u in halves]
+        x_codes = [keep.tile([P, BANK], U32, name="x_codes%d" % u, align_bytes=64) for u in halves]
+        for u in halves:
+            nc.vector.tensor_copy(x_bytes[u][:], x_byte_table[:].indirect(entries(offs_l, u * BANK, (u + 1) * BANK)))
+        for u in halves:
+            nc.vector.tensor_copy(x_codes[u][:], x_word_table[:].bitcast(U32).indirect(entries(offs_l, u * BANK, (u + 1) * BANK)))
+        for t0 in (0, 2):
+            order = [(t, u) for u in halves for t in (t0, t0 + 1)] if t0 == 0 else [(t, u) for t in (t0, t0 + 1) for u in halves]
+            for t, u in order:
                 acc = psum.tile([P, BANK], F32, name="acc")
-                multiply(acc[:], w1_words, w1_scales, t, x_codes[:], x_bytes[:])
+                multiply(acc[:], w1_words, w1_scales, t, x_codes[u][:], x_bytes[u][:])
                 nc.scalar.activation(h[t][:, u * BANK : (u + 1) * BANK], acc[:], ACT.Copy, scale=SIXTEENTH)
 
-        w2_scales = pick_bytes("w2_scales", k2_l, "x_word_table")
+        w2_scales = place("w2_scales", deal("w2_bytes", pick("w2_bytes_picked", d_byte_table[:], U8, k2_l, "x_word_table"), U8, 16))
 
         z_bf = []
         for c, (v0, v1) in enumerate(Z_CHUNKS):
             n = v1 - v0
-            lined_a = keep.tile([P, PACK - 1, 2 * n], F32, name="lined_a%d" % c, tag="lined_a")
-            lined_b = keep.tile([P, 1, 2 * n], F32, name="lined_b%d" % c, tag="lined_b")
             larger = keep.tile([P, PACK, n], F32, name="larger%d" % c, tag="larger%d" % c, align_bytes=64)
             z_rows = keep.tile([P, PACK, n], BF16, name="z_rows%d" % c)
-            z_woven = keep.tile([P, n, PACK], BF16, name="z_woven%d" % c, align_bytes=64)
-            for t in range(PACK):
-                dst = lined_a[:, t, :] if t < PACK - 1 else lined_b[:, 0, :]
-                nc.vector.tensor_copy(dst, h[t][:].indirect(entries(n1_l, 2 * v0, 2 * v1)))
-            for part, rows in ((lined_a, slice(0, PACK - 1)), (lined_b, slice(PACK - 1, PACK))):
-                pairs = part[:].rearrange("p t (v e) -> p (t v) e", e=2)
-                nc.vector.tensor_tensor(larger[:, rows, :].rearrange("p t v -> p (t v)"), pairs[:, :, 0], pairs[:, :, 1], ALU.max)
+            z_woven = keep.tile([P, n, PACK], BF16, name="z_woven%d" % c, tag="z_woven%d" % c, align_bytes=64)
+            for pair in range(2):
+                lined = keep.tile([P, 2, 2 * n], F32, name="lined%d_%d" % (c, pair), tag="lined%d" % ((c + pair) % 2))
+                for e in range(2):
+                    nc.vector.tensor_copy(lined[:, e, :], h[2 * pair + e][:].indirect(entries(n1_l, 2 * v0, 2 * v1)))
+                both = lined[:].rearrange("p t (v e) -> p (t v) e", e=2)
+                nc.vector.tensor_tensor(
+                    larger[:, 2 * pair : 2 * pair + 2, :].rearrange("p t v -> p (t v)"), both[:, :, 0], both[:, :, 1], ALU.max
+                )
             for t in range(PACK):
                 nc.scalar.activation(z_rows[:, t, :], larger[:, t, :], ACT.Copy, scale=gain[:, t : t + 1])
             nc.scalar.copy(
@@ -134,93 +135,113 @@ def tile_picked_codepoollerp_none_po_kernel(tc, x_words, x_scales, d_words, d_sc
             )
             z_bf.append(z_woven)
 
-        w2_words = pick_words("w2_words", k2_l, "larger1")
-
         z_codes = keep.tile([P, V], U32, align_bytes=64)
         z_bytes = keep.tile([P, V], U8, align_bytes=64)
-        for c, (v0, v1) in enumerate(Z_CHUNKS):
+
+        def quantise_z(c):
+            v0, v1 = Z_CHUNKS[c]
             nc.vector.quantize_mx(
                 out=z_codes[:, v0:v1].bitcast(FP8X4), scales=z_bytes[:, v0:v1],
                 in_=z_bf[c][:].rearrange("p v t -> p (v t)"),
             )
 
-        h2 = [keep.tile([P, V], F32, name="h2_%d" % t) for t in range(PACK)]
+        quantise_z(0)
+        w2_words = deal("w2_words", pick("w2_words_picked", d_word_table[:].bitcast(U32), U32, k2_l, "z_woven0"), U32, 4)
 
-        def second_layer(t):
-            for group in (Z_CHUNKS[:-1], Z_CHUNKS[-1:]):
-                acc = psum.tile([P, BANK], F32, name="acc")
-                for v0, v1 in group:
-                    multiply(acc[:, v0:v1], w2_words, w2_scales, t, z_codes[:, v0:v1], z_bytes[:, v0:v1])
-                cols = slice(group[0][0], group[-1][1])
-                nc.scalar.activation(h2[t][:, cols], acc[:, cols], ACT.Copy, scale=SIXTEENTH)
+        quantise_z(1)
+
+        h2 = [keep.tile([P, 2 * V], F32, name="h2_%d" % t) for t in range(PACK)]
+        for t in range(PACK):
+            nc.gpsimd.memset(h2[t][:, V:], 0.0)
+
+        def second_layer(t, cols, empty):
+            acc = psum.tile([P, BANK], F32, name="acc")
+            multiply(acc[:, cols], w2_words, w2_scales, t, z_codes[:, cols], z_bytes[:, cols])
+            empty(h2[t][:, cols], acc[:, cols], SIXTEENTH)
 
         out_rows = out_0.rearrange("(p t) v -> p t v", t=PACK)
         out_words = out_1[0].rearrange("p c r -> p (c r)").bitcast(I32)
         out_bytes = keep.tile([P, V], U8, align_bytes=64)
-        def chunk_tiles(name, dtype):
-            return [keep.tile([P, PACK, v1 - v0], dtype, name="%s%d" % (name, c), align_bytes=64) for c, (v0, v1) in enumerate(OUT_CHUNKS)]
+        codes = keep.tile([P, V], U32, align_bytes=64)
+        gate, rest, far, near, mixed = (keep.tile([P, PACK, V], F32, name=name) for name in ("gate", "rest", "far", "near", "mixed"))
+        woven = keep.tile([P, V * PACK], BF16, align_bytes=64)
 
-        gate, rest, far, near, mixed = (chunk_tiles(name, F32) for name in ("gate", "rest", "far", "near", "mixed"))
-        woven = chunk_tiles("woven", BF16)
+        def gates(t):
+            nc.scalar.activation(gate[:, t, :], h2[t][:].indirect(n3_l[:]), ACT.Sigmoid)
 
-        def fetch(c, t):
-            v0, v1 = OUT_CHUNKS[c]
-            nc.scalar.activation(gate[c][:, t, :], h2[t][:].indirect(entries(n3_l, v0, v1)), ACT.Sigmoid)
-            nc.scalar.activation(rest[c][:, t, :], gate[c][:, t, :], ACT.Copy, scale=-1.0, bias=1.0)
-            nc.vector.tensor_tensor(far[c][:, t, :], h2[t][:].indirect(entries(n4_l, v0, v1)), gate[c][:, t, :], ALU.mult)
-            nc.vector.tensor_tensor(near[c][:, t, :], h2[t][:].indirect(entries(n2_l, v0, v1)), rest[c][:, t, :], ALU.mult)
+        def rests(t):
+            nc.scalar.activation(rest[:, t, :], gate[:, t, :], ACT.Copy, scale=-1.0, bias=1.0)
 
-        def fetch_first(c, t):
-            v0, v1 = OUT_CHUNKS[c]
-            step = keep.tile([P, v1 - v0], F32)
-            nc.scalar.activation(gate[c][:, t, :], h2[t][:].indirect(entries(n3_l, v0, v1)), ACT.Sigmoid)
-            nc.vector.tensor_copy(near[c][:, t, :], h2[t][:].indirect(entries(n2_l, v0, v1)))
-            nc.vector.tensor_tensor(step[:], h2[t][:].indirect(entries(n4_l, v0, v1)), near[c][:, t, :], ALU.subtract)
-            nc.vector.tensor_tensor(far[c][:, t, :], step[:], gate[c][:, t, :], ALU.mult)
+        def fetch(t, cols):
+            nc.vector.tensor_tensor(far[:, t, cols], h2[t][:].indirect(entries(n4_l, cols.start, cols.stop)), gate[:, t, cols], ALU.mult)
+            nc.vector.tensor_tensor(near[:, t, cols], h2[t][:].indirect(entries(n2_l, cols.start, cols.stop)), rest[:, t, cols], ALU.mult)
 
-        def mix(c, t0, count=2):
-            v0, v1 = OUT_CHUNKS[c]
-            rows = slice(t0, t0 + count)
-            nc.vector.tensor_tensor(mixed[c][:, rows, :], near[c][:, rows, :], far[c][:, rows, :], ALU.add)
-            nc.sync.dma_start(out_rows[:, rows, v0:v1], mixed[c][:, rows, :])
+        def fetch_first(t):
+            step = keep.tile([P, V], F32)
+            nc.vector.tensor_copy(near[:, t, :], h2[t][:].indirect(n2_l[:]))
+            nc.vector.tensor_tensor(step[:], h2[t][:].indirect(n4_l[:]), near[:, t, :], ALU.subtract)
+            nc.vector.tensor_tensor(far[:, t, :], step[:], gate[:, t, :], ALU.mult)
 
-        def weave(c, copy, quads):
+        def add(rows, cols):
+            nc.vector.tensor_tensor(mixed[:, rows, cols], near[:, rows, cols], far[:, rows, cols], ALU.add)
+
+        def store(rows, cols):
+            nc.sync.dma_start(out_rows[:, rows, cols], mixed[:, rows, cols])
+
+        def weave(copy, cols):
+            quads = slice(cols.start // 4, cols.stop // 4)
             copy(
-                woven[c][:].rearrange("p t v -> p (t v)").rearrange("p (c i t) -> p c t i", i=4, t=PACK)[:, quads],
-                mixed[c][:].rearrange("p t (c i) -> p c t i", i=4)[:, quads],
+                woven[:].rearrange("p (c i t) -> p c t i", i=4, t=PACK)[:, quads],
+                mixed[:].rearrange("p t (c i) -> p c t i", i=4)[:, quads],
             )
 
-        def hand_on(c):
-            v0, v1 = OUT_CHUNKS[c]
-            codes = keep.tile([P, v1 - v0], U32, name="codes%d" % c, align_bytes=64)
+        def quantise(cols):
             nc.vector.quantize_mx(
-                out=codes[:].bitcast(FP8X4), scales=out_bytes[:, v0:v1],
-                in_=woven[c][:].rearrange("p t v -> p (t v)"),
+                out=codes[:, cols].bitcast(FP8X4), scales=out_bytes[:, cols],
+                in_=woven[:, PACK * cols.start : PACK * cols.stop],
             )
-            nc.sync.dma_start(out_words[:, v0:v1], codes[:].bitcast(I32))
 
-        second_layer(0)
-        fetch_first(0, 0)
-        second_layer(1)
-        fetch(1, 0)
-        fetch(0, 1)
-        second_layer(2)
-        fetch(1, 1)
-        mix(0, 0)
-        fetch(0, 2)
-        second_layer(3)
-        mix(1, 0)
-        fetch(0, 3)
-        fetch(1, 2)
-        mix(0, 2)
-        mix(1, 2, 1)
-        fetch(1, 3)
-        weave(0, nc.scalar.copy, slice(0, 64))
-        mix(1, 3, 1)
-        hand_on(0)
-        weave(1, nc.scalar.copy, slice(0, 24))
-        weave(1, nc.vector.tensor_copy, slice(24, 64))
-        hand_on(1)
+        def store_codes(cols):
+            nc.sync.dma_start(out_words[:, cols], codes[:, cols].bitcast(I32))
+
+        whole, first, second = slice(0, V), slice(0, V // 2), slice(V // 2, V)
+        parts = (slice(256, 384), slice(384, 512))
+        second_layer(0, first, nc.scalar.mul)
+        second_layer(0, second, nc.vector.tensor_scalar_mul)
+        gates(0)
+        second_layer(1, whole, nc.scalar.mul)
+        fetch_first(0)
+        gates(1)
+        rests(1)
+        second_layer(2, whole, nc.scalar.mul)
+        fetch(1, whole)
+        gates(2)
+        rests(2)
+        second_layer(3, whole, nc.scalar.mul)
+        add(slice(0, 1), whole)
+        store(slice(0, 1), whole)
+        fetch(2, whole)
+        add(slice(1, 2), whole)
+        store(slice(1, 2), whole)
+        gates(3)
+        rests(3)
+        fetch(3, first)
+        add(slice(2, 3), whole)
+        store(slice(2, 3), whole)
+        add(slice(3, 4), first)
+        store(slice(3, 4), first)
+        fetch(3, second)
+        weave(nc.scalar.copy, first)
+        for cols in parts:
+            add(slice(3, 4), cols)
+        store(slice(3, 4), second)
+        for cols in parts:
+            weave(nc.vector.tensor_copy, cols)
+        quantise(first)
+        store_codes(first)
+        for cols in parts:
+            quantise(cols)
+        store_codes(second)
         for q in range(4):
             queue = nc.scalar if q % 2 else nc.sync
             queue.dma_start(out_2[0].bitcast(I32)[4 * q : 4 * q + 4, :], out_bytes[:].bitcast(I32)[32 * q : 32 * q + 4, :])

@@ -12,25 +12,44 @@ FP8X4 = mybir.dt.float8_e4m3fn_x4
 ALU = mybir.AluOpType
 ACT = mybir.ActivationFunctionType
 
-P = 128
-PACK = 4
 K, T, S, V, G, H = 512, 2048, 1024, 512, 2048, 512
-BANK = 512
-SIXTEENTH = 0.0625
 FLOPS = 2 * K * H * S + 2 * K * H * V
 
-Z_CHUNKS = ((0, 256), (256, 512))
+P = 128
+PACK = 4
+GROUP = 16
+QUADRANT = 32
+BLOCK_PARTITIONS = 8
+BANK = 512
+BANKS = 8
+LINE = 16
+WEAVE_RUN = 4
+SIXTEENTH = 0.0625
+
+WHOLE = slice(0, V)
+HALVES = (slice(0, V // 2), slice(V // 2, V))
+LAST_QUARTERS = (slice(V // 2, 3 * V // 4), slice(3 * V // 4, V))
 
 
-def entries(lists, first, last):
-    return lists[:, first // 16 : last // 16]
+def entries(lists, cols):
+    return lists[:, cols.start // GROUP : cols.stop // GROUP]
 
 
-def tile_picked_codepoollerp_none_po_kernel(tc, x_words, x_scales, d_words, d_scales, gs, offs, k1, n1, k2, n2, n3, n4, out_0, out_1, out_2):
+def weave(copy, woven, rows, cols):
+    runs = slice(cols.start // WEAVE_RUN, cols.stop // WEAVE_RUN)
+    copy(
+        woven[:].rearrange("p (c i t) -> p c t i", i=WEAVE_RUN, t=PACK)[:, runs],
+        rows[:].rearrange("p t (c i) -> p c t i", i=WEAVE_RUN)[:, runs],
+    )
+
+
+def tile_picked_codepoollerp_none_po_kernel(
+    tc, x_words, x_scales, d_words, d_scales, gs, offs, k1, n1, k2, n2, n3, n4, out_0, out_1, out_2
+):
     nc = tc.nc
     with ExitStack() as ctx:
         keep = ctx.enter_context(tc.tile_pool(name="keep", bufs=1))
-        psum = ctx.enter_context(tc.psum_pool(name="psum", bufs=8))
+        psum = ctx.enter_context(tc.psum_pool(name="psum", bufs=BANKS))
 
         def load_list(name, src):
             lists = keep.tile(list(src.shape), U16, name=name)
@@ -50,19 +69,23 @@ def tile_picked_codepoollerp_none_po_kernel(tc, x_words, x_scales, d_words, d_sc
         warm = keep.tile([P, 1], F32, tag="x_word_table", align_bytes=64)
         nc.gpsimd.memset(warm[:], 0.0)
         nc.scalar.activation(warm[:], warm[:], ACT.Sigmoid)
+
         d_word_table = load_words("d_word_table", d_words, nc.sync)
-        k1_l = load_list("k1_l", k1)
-        offs_l = load_list("offs_l", offs)
-        k2_l = load_list("k2_l", k2)
-        n1_l = load_list("n1_l", n1)
-        n3_l = load_list("n3_l", n3)
-        n4_l = load_list("n4_l", n4)
-        n2_l = load_list("n2_l", n2)
+        k1_list = load_list("k1_list", k1)
+        offs_list = load_list("offs_list", offs)
+        k2_list = load_list("k2_list", k2)
+        n1_list = load_list("n1_list", n1)
+        n3_list = load_list("n3_list", n3)
+        n4_list = load_list("n4_list", n4)
+        n2_list = load_list("n2_list", n2)
         gain = keep.tile([P, PACK], F32)
         nc.scalar.dma_start(gain[:], gs.rearrange("(p t) o -> p (t o)", t=PACK))
-        nc.scalar.dma_start(d_byte_table[:].bitcast(I32)[0:P:8, :], d_scales[0].bitcast(I32))
-        for q in range(4):
-            nc.scalar.dma_start(x_byte_table[:].bitcast(I32)[32 * q : 32 * q + 4, :], x_scales[0].bitcast(I32)[4 * q : 4 * q + 4, :])
+        nc.scalar.dma_start(d_byte_table[:].bitcast(I32)[0:P:BLOCK_PARTITIONS, :], d_scales[0].bitcast(I32))
+        for q in range(P // QUADRANT):
+            nc.scalar.dma_start(
+                x_byte_table[:].bitcast(I32)[QUADRANT * q : QUADRANT * q + PACK, :],
+                x_scales[0].bitcast(I32)[PACK * q : PACK * (q + 1), :],
+            )
         x_word_table = load_words("x_word_table", x_words, nc.scalar)
 
         def pick(name, table, dtype, lists, tag):
@@ -70,178 +93,181 @@ def tile_picked_codepoollerp_none_po_kernel(tc, x_words, x_scales, d_words, d_sc
             nc.vector.tensor_copy(picked[:], table.indirect(lists[:]))
             return picked
 
+        def deal_tiles(dealt, picked, run, tiles):
+            nc.vector.tensor_copy(
+                dealt[:].rearrange("p (t c i) -> p c t i", t=PACK, i=run)[:, :, tiles, :],
+                picked[:].rearrange("p (c i t) -> p c t i", t=PACK, i=run)[:, :, tiles, :],
+            )
+
         def deal(name, picked, dtype, run):
             dealt = keep.tile([P, H], dtype, name=name, align_bytes=64)
-            nc.vector.tensor_copy(
-                dealt[:].rearrange("p (t c i) -> p c t i", t=PACK, i=run),
-                picked[:].rearrange("p (c i t) -> p c t i", t=PACK, i=run),
-            )
+            deal_tiles(dealt, picked, run, slice(0, PACK))
             return dealt
 
         def place(name, dealt):
             placed = keep.tile([P, H], U8, name=name, align_bytes=64)
             nc.gpsimd.memset(placed[:].bitcast(I32), 0)
-            for q in range(4):
-                nc.sync.dma_start(placed[:].bitcast(I32)[32 * q : 32 * q + 4, :], dealt[:].bitcast(I32)[32 * q : 32 * q + 32 : 8, :])
+            for q in range(P // QUADRANT):
+                nc.sync.dma_start(
+                    placed[:].bitcast(I32)[QUADRANT * q : QUADRANT * q + PACK, :],
+                    dealt[:].bitcast(I32)[QUADRANT * q : QUADRANT * (q + 1) : BLOCK_PARTITIONS, :],
+                )
             return placed
 
-        def multiply(out, words, scales, t, rhs_words, rhs_scales):
-            cols = slice(t * P, (t + 1) * P)
+        def multiply(out, w_words, w_scales, t, rhs_words, rhs_scales):
+            features = slice(t * P, (t + 1) * P)
             nc.tensor.matmul_mx(
-                out=out, lhsT=words[:, cols].bitcast(FP8X4), lhsT_scale=scales[:, cols],
-                rhs=rhs_words.bitcast(FP8X4), rhs_scale=rhs_scales, start=True, stop=True,
+                out=out,
+                lhsT=w_words[:, features].bitcast(FP8X4),
+                lhsT_scale=w_scales[:, features],
+                rhs=rhs_words.bitcast(FP8X4),
+                rhs_scale=rhs_scales,
+                start=True,
+                stop=True,
             )
 
-        w1_words_picked = pick("w1_words_picked", d_word_table[:].bitcast(U32), U32, k1_l, "w1_words_picked")
-        w1_bytes_picked = pick("w1_bytes_picked", d_byte_table[:], U8, k1_l, "w1_bytes_picked")
-        w1_words = deal("w1_words", w1_words_picked, U32, 4)
-        w1_scales = place("w1_scales", deal("w1_bytes", w1_bytes_picked, U8, 16))
+        def quantise(codes, scales, woven, cols):
+            nc.vector.quantize_mx(
+                out=codes[:, cols].bitcast(FP8X4),
+                scales=scales[:, cols],
+                in_=woven[:, PACK * cols.start : PACK * cols.stop],
+            )
+
+        word_run, byte_run = LINE // 4, LINE
+        w1_words_picked = pick("w1_words_picked", d_word_table[:].bitcast(U32), U32, k1_list, "w1_words_picked")
+        w1_bytes_picked = pick("w1_bytes_picked", d_byte_table[:], U8, k1_list, "w1_bytes_picked")
+        w1_words = deal("w1_words", w1_words_picked, U32, word_run)
+        w1_scales = place("w1_scales", deal("w1_bytes", w1_bytes_picked, U8, byte_run))
+
+        token_banks = [slice(u * BANK, (u + 1) * BANK) for u in range(S // BANK)]
+        x_bytes = [keep.tile([P, BANK], U8, name="x_bytes%d" % u, align_bytes=64) for u in range(S // BANK)]
+        x_codes = [keep.tile([P, BANK], U32, name="x_codes%d" % u, align_bytes=64) for u in range(S // BANK)]
+        for u, tokens in enumerate(token_banks):
+            nc.vector.tensor_copy(x_bytes[u][:], x_byte_table[:].indirect(entries(offs_list, tokens)))
+        for u, tokens in enumerate(token_banks):
+            nc.vector.tensor_copy(x_codes[u][:], x_word_table[:].bitcast(U32).indirect(entries(offs_list, tokens)))
+
         h = [keep.tile([P, S], F32, name="h%d" % t) for t in range(PACK)]
-        halves = range(S // BANK)
-        x_bytes = [keep.tile([P, BANK], U8, name="x_bytes%d" % u, align_bytes=64) for u in halves]
-        x_codes = [keep.tile([P, BANK], U32, name="x_codes%d" % u, align_bytes=64) for u in halves]
-        for u in halves:
-            nc.vector.tensor_copy(x_bytes[u][:], x_byte_table[:].indirect(entries(offs_l, u * BANK, (u + 1) * BANK)))
-        for u in halves:
-            nc.vector.tensor_copy(x_codes[u][:], x_word_table[:].bitcast(U32).indirect(entries(offs_l, u * BANK, (u + 1) * BANK)))
-        for t0 in (0, 2):
-            order = [(t, u) for u in halves for t in (t0, t0 + 1)] if t0 == 0 else [(t, u) for t in (t0, t0 + 1) for u in halves]
-            for t, u in order:
-                acc = psum.tile([P, BANK], F32, name="acc")
-                multiply(acc[:], w1_words, w1_scales, t, x_codes[u][:], x_bytes[u][:])
-                nc.scalar.activation(h[t][:, u * BANK : (u + 1) * BANK], acc[:], ACT.Copy, scale=SIXTEENTH)
+        order = [(t, u) for u in range(S // BANK) for t in (0, 1)] + [(t, u) for t in (2, 3) for u in range(S // BANK)]
+        for t, u in order:
+            acc = psum.tile([P, BANK], F32, name="acc")
+            multiply(acc[:], w1_words, w1_scales, t, x_codes[u][:], x_bytes[u][:])
+            nc.scalar.activation(h[t][:, token_banks[u]], acc[:], ACT.Copy, scale=SIXTEENTH)
 
-        w2_scales = place("w2_scales", deal("w2_bytes", pick("w2_bytes_picked", d_byte_table[:], U8, k2_l, "x_word_table"), U8, 16))
+        w2_bytes_picked = pick("w2_bytes_picked", d_byte_table[:], U8, k2_list, "x_word_table")
+        w2_scales = place("w2_scales", deal("w2_bytes", w2_bytes_picked, U8, byte_run))
 
-        z_bf = []
-        for c, (v0, v1) in enumerate(Z_CHUNKS):
-            n = v1 - v0
-            larger = keep.tile([P, PACK, n], F32, name="larger%d" % c, tag="larger%d" % c, align_bytes=64)
-            z_rows = keep.tile([P, PACK, n], BF16, name="z_rows%d" % c)
-            z_woven = keep.tile([P, n, PACK], BF16, name="z_woven%d" % c, tag="z_woven%d" % c, align_bytes=64)
-            for pair in range(2):
-                lined = keep.tile([P, 2, 2 * n], F32, name="lined%d_%d" % (c, pair), tag="lined%d" % ((c + pair) % 2))
+        z_woven = keep.tile([P, V * PACK], BF16, align_bytes=64)
+        for c, cols in enumerate(HALVES):
+            n = cols.stop - cols.start
+            larger = keep.tile([P, PACK, n], F32, name="larger%d" % c)
+            z_rows = keep.tile([P, PACK, n], BF16, name="z_rows%d" % c, tag="z_rows%d" % c, align_bytes=64)
+            for two in range(PACK // 2):
+                lined = keep.tile([P, 2, 2 * n], F32, name="lined%d_%d" % (c, two), tag="lined%d" % ((c + two) % 2))
                 for e in range(2):
-                    nc.vector.tensor_copy(lined[:, e, :], h[2 * pair + e][:].indirect(entries(n1_l, 2 * v0, 2 * v1)))
-                both = lined[:].rearrange("p t (v e) -> p (t v) e", e=2)
-                nc.vector.tensor_tensor(
-                    larger[:, 2 * pair : 2 * pair + 2, :].rearrange("p t v -> p (t v)"), both[:, :, 0], both[:, :, 1], ALU.max
-                )
+                    neighbours = entries(n1_list, slice(2 * cols.start, 2 * cols.stop))
+                    nc.vector.tensor_copy(lined[:, e, :], h[2 * two + e][:].indirect(neighbours))
+                pairs = lined[:].rearrange("p t (v n) -> p t v n", n=2)
+                for e in range(2):
+                    nc.vector.tensor_tensor(larger[:, 2 * two + e, :], pairs[:, e, :, 0], pairs[:, e, :, 1], ALU.max)
             for t in range(PACK):
                 nc.scalar.activation(z_rows[:, t, :], larger[:, t, :], ACT.Copy, scale=gain[:, t : t + 1])
-            nc.scalar.copy(
-                z_woven[:].rearrange("p (c i) t -> p c t i", i=4),
-                z_rows[:].rearrange("p t (c i) -> p c t i", i=4),
-            )
-            z_bf.append(z_woven)
+            weave(nc.scalar.copy, z_woven[:, PACK * cols.start : PACK * cols.stop], z_rows, slice(0, n))
 
         z_codes = keep.tile([P, V], U32, align_bytes=64)
         z_bytes = keep.tile([P, V], U8, align_bytes=64)
-
-        def quantise_z(c):
-            v0, v1 = Z_CHUNKS[c]
-            nc.vector.quantize_mx(
-                out=z_codes[:, v0:v1].bitcast(FP8X4), scales=z_bytes[:, v0:v1],
-                in_=z_bf[c][:].rearrange("p v t -> p (v t)"),
-            )
-
-        quantise_z(0)
-        w2_words = deal("w2_words", pick("w2_words_picked", d_word_table[:].bitcast(U32), U32, k2_l, "z_woven0"), U32, 4)
-
-        quantise_z(1)
+        w2_words_picked = pick("w2_words_picked", d_word_table[:].bitcast(U32), U32, k2_list, "z_rows0")
+        quantise(z_codes, z_bytes, z_woven, HALVES[0])
+        w2_words = keep.tile([P, H], U32, align_bytes=64)
+        deal_tiles(w2_words, w2_words_picked, word_run, slice(0, 1))
+        quantise(z_codes, z_bytes, z_woven, HALVES[1])
 
         h2 = [keep.tile([P, 2 * V], F32, name="h2_%d" % t) for t in range(PACK)]
         for t in range(PACK):
             nc.gpsimd.memset(h2[t][:, V:], 0.0)
 
-        def second_layer(t, cols, empty):
+        def second_layer(t, cols, copy_out):
             acc = psum.tile([P, BANK], F32, name="acc")
             multiply(acc[:, cols], w2_words, w2_scales, t, z_codes[:, cols], z_bytes[:, cols])
-            empty(h2[t][:, cols], acc[:, cols], SIXTEENTH)
+            copy_out(h2[t][:, cols], acc[:, cols], SIXTEENTH)
 
+        gate, rest, far, near, mixed = (
+            keep.tile([P, PACK, V], F32, name=name) for name in ("gate", "rest", "far", "near", "mixed")
+        )
+        out_woven = keep.tile([P, V * PACK], BF16, align_bytes=64)
+        out_codes = keep.tile([P, V], U32, align_bytes=64)
+        out_bytes = keep.tile([P, V], U8, align_bytes=64)
         out_rows = out_0.rearrange("(p t) v -> p t v", t=PACK)
         out_words = out_1[0].rearrange("p c r -> p (c r)").bitcast(I32)
-        out_bytes = keep.tile([P, V], U8, align_bytes=64)
-        codes = keep.tile([P, V], U32, align_bytes=64)
-        gate, rest, far, near, mixed = (keep.tile([P, PACK, V], F32, name=name) for name in ("gate", "rest", "far", "near", "mixed"))
-        woven = keep.tile([P, V * PACK], BF16, align_bytes=64)
 
-        def gates(t):
-            nc.scalar.activation(gate[:, t, :], h2[t][:].indirect(n3_l[:]), ACT.Sigmoid)
+        def fetch_gate(t, cols):
+            nc.scalar.activation(gate[:, t, cols], h2[t][:].indirect(entries(n3_list, cols)), ACT.Sigmoid)
 
-        def rests(t):
-            nc.scalar.activation(rest[:, t, :], gate[:, t, :], ACT.Copy, scale=-1.0, bias=1.0)
+        def fetch_weights(t, cols):
+            fetch_gate(t, cols)
+            nc.scalar.activation(rest[:, t, cols], gate[:, t, cols], ACT.Copy, scale=-1.0, bias=1.0)
 
-        def fetch(t, cols):
-            nc.vector.tensor_tensor(far[:, t, cols], h2[t][:].indirect(entries(n4_l, cols.start, cols.stop)), gate[:, t, cols], ALU.mult)
-            nc.vector.tensor_tensor(near[:, t, cols], h2[t][:].indirect(entries(n2_l, cols.start, cols.stop)), rest[:, t, cols], ALU.mult)
+        def fetch_terms(t, cols):
+            nc.vector.tensor_tensor(
+                far[:, t, cols], h2[t][:].indirect(entries(n4_list, cols)), gate[:, t, cols], ALU.mult
+            )
+            nc.vector.tensor_tensor(
+                near[:, t, cols], h2[t][:].indirect(entries(n2_list, cols)), rest[:, t, cols], ALU.mult
+            )
 
-        def fetch_first(t):
+        def fetch_terms_before_gate(t):
             step = keep.tile([P, V], F32)
-            nc.vector.tensor_copy(near[:, t, :], h2[t][:].indirect(n2_l[:]))
-            nc.vector.tensor_tensor(step[:], h2[t][:].indirect(n4_l[:]), near[:, t, :], ALU.subtract)
-            nc.vector.tensor_tensor(far[:, t, :], step[:], gate[:, t, :], ALU.mult)
+            for cols in HALVES:
+                nc.vector.tensor_copy(near[:, t, cols], h2[t][:].indirect(entries(n2_list, cols)))
+            for cols in HALVES:
+                nc.vector.tensor_tensor(
+                    step[:, cols], h2[t][:].indirect(entries(n4_list, cols)), near[:, t, cols], ALU.subtract
+                )
+            for cols in HALVES:
+                nc.vector.tensor_tensor(far[:, t, cols], step[:, cols], gate[:, t, cols], ALU.mult)
 
-        def add(rows, cols):
-            nc.vector.tensor_tensor(mixed[:, rows, cols], near[:, rows, cols], far[:, rows, cols], ALU.add)
+        def add(t, cols):
+            nc.vector.tensor_tensor(mixed[:, t, cols], near[:, t, cols], far[:, t, cols], ALU.add)
 
-        def store(rows, cols):
-            nc.sync.dma_start(out_rows[:, rows, cols], mixed[:, rows, cols])
+        def store(t, cols):
+            nc.sync.dma_start(out_rows[:, t, cols], mixed[:, t, cols])
 
-        def weave(copy, cols):
-            quads = slice(cols.start // 4, cols.stop // 4)
-            copy(
-                woven[:].rearrange("p (c i t) -> p c t i", i=4, t=PACK)[:, quads],
-                mixed[:].rearrange("p t (c i) -> p c t i", i=4)[:, quads],
-            )
+        def hand_on(cols):
+            quantise(out_codes, out_bytes, out_woven, cols)
+            nc.sync.dma_start(out_words[:, cols], out_codes[:, cols].bitcast(I32))
 
-        def quantise(cols):
-            nc.vector.quantize_mx(
-                out=codes[:, cols].bitcast(FP8X4), scales=out_bytes[:, cols],
-                in_=woven[:, PACK * cols.start : PACK * cols.stop],
-            )
-
-        def store_codes(cols):
-            nc.sync.dma_start(out_words[:, cols], codes[:, cols].bitcast(I32))
-
-        whole, first, second = slice(0, V), slice(0, V // 2), slice(V // 2, V)
-        parts = (slice(256, 384), slice(384, 512))
-        second_layer(0, first, nc.scalar.mul)
-        second_layer(0, second, nc.vector.tensor_scalar_mul)
-        gates(0)
-        second_layer(1, whole, nc.scalar.mul)
-        fetch_first(0)
-        gates(1)
-        rests(1)
-        second_layer(2, whole, nc.scalar.mul)
-        fetch(1, whole)
-        gates(2)
-        rests(2)
-        second_layer(3, whole, nc.scalar.mul)
-        add(slice(0, 1), whole)
-        store(slice(0, 1), whole)
-        fetch(2, whole)
-        add(slice(1, 2), whole)
-        store(slice(1, 2), whole)
-        gates(3)
-        rests(3)
-        fetch(3, first)
-        add(slice(2, 3), whole)
-        store(slice(2, 3), whole)
-        add(slice(3, 4), first)
-        store(slice(3, 4), first)
-        fetch(3, second)
-        weave(nc.scalar.copy, first)
-        for cols in parts:
-            add(slice(3, 4), cols)
-        store(slice(3, 4), second)
-        for cols in parts:
-            weave(nc.vector.tensor_copy, cols)
-        quantise(first)
-        store_codes(first)
-        for cols in parts:
-            quantise(cols)
-        store_codes(second)
-        for q in range(4):
+        second_layer(0, HALVES[0], nc.scalar.mul)
+        deal_tiles(w2_words, w2_words_picked, word_run, slice(1, PACK))
+        second_layer(0, HALVES[1], nc.vector.tensor_scalar_mul)
+        fetch_gate(0, WHOLE)
+        second_layer(1, WHOLE, nc.scalar.mul)
+        fetch_terms_before_gate(0)
+        last = PACK - 1
+        for t in range(1, last):
+            fetch_weights(t, WHOLE)
+            second_layer(t + 1, WHOLE, nc.scalar.mul)
+            fetch_terms(t, WHOLE)
+            add(t - 1, WHOLE)
+            store(t - 1, WHOLE)
+        add(last - 1, WHOLE)
+        store(last - 1, WHOLE)
+        for cols in HALVES:
+            fetch_weights(last, cols)
+        fetch_terms(last, HALVES[0])
+        add(last, HALVES[0])
+        store(last, HALVES[0])
+        fetch_terms(last, HALVES[1])
+        weave(nc.scalar.copy, out_woven, mixed, HALVES[0])
+        for cols in LAST_QUARTERS:
+            add(last, cols)
+        store(last, HALVES[1])
+        weave(nc.scalar.copy, out_woven, mixed, LAST_QUARTERS[0])
+        hand_on(HALVES[0])
+        weave(nc.vector.tensor_copy, out_woven, mixed, LAST_QUARTERS[1])
+        hand_on(HALVES[1])
+        for q in range(P // QUADRANT):
             queue = nc.scalar if q % 2 else nc.sync
-            queue.dma_start(out_2[0].bitcast(I32)[4 * q : 4 * q + 4, :], out_bytes[:].bitcast(I32)[32 * q : 32 * q + 4, :])
+            queue.dma_start(
+                out_2[0].bitcast(I32)[PACK * q : PACK * (q + 1), :],
+                out_bytes[:].bitcast(I32)[QUADRANT * q : QUADRANT * q + PACK, :],
+            )

from contextlib import ExitStack

import concourse.mybir as mybir

F32 = mybir.dt.float32
BF16 = mybir.dt.bfloat16
I32 = mybir.dt.int32
U32 = mybir.dt.uint32
U16 = mybir.dt.uint16
U8 = mybir.dt.uint8
FP8X4 = mybir.dt.float8_e4m3fn_x4
ALU = mybir.AluOpType
ACT = mybir.ActivationFunctionType

K, T, S, V, G, H = 512, 2048, 1024, 512, 2048, 512
FLOPS = 2 * K * H * S + 2 * K * H * V

P = 128
PACK = 4
GROUP = 16
QUADRANT = 32
BLOCK_PARTITIONS = 8
BANK = 512
BANKS = 8
LINE = 16
WEAVE_RUN = 4
SIXTEENTH = 0.0625

WHOLE = slice(0, V)
HALVES = (slice(0, V // 2), slice(V // 2, V))
LAST_QUARTERS = (slice(V // 2, 3 * V // 4), slice(3 * V // 4, V))


def entries(lists, cols):
    return lists[:, cols.start // GROUP : cols.stop // GROUP]


def weave(copy, woven, rows, cols):
    runs = slice(cols.start // WEAVE_RUN, cols.stop // WEAVE_RUN)
    copy(
        woven[:].rearrange("p (c i t) -> p c t i", i=WEAVE_RUN, t=PACK)[:, runs],
        rows[:].rearrange("p t (c i) -> p c t i", i=WEAVE_RUN)[:, runs],
    )


def tile_picked_codepoollerp_none_po_kernel(
    tc, x_words, x_scales, d_words, d_scales, gs, offs, k1, n1, k2, n2, n3, n4, out_0, out_1, out_2
):
    nc = tc.nc
    with ExitStack() as ctx:
        keep = ctx.enter_context(tc.tile_pool(name="keep", bufs=1))
        psum = ctx.enter_context(tc.psum_pool(name="psum", bufs=BANKS))

        def load_list(name, src):
            lists = keep.tile(list(src.shape), U16, name=name)
            nc.sync.dma_start(lists[:], src)
            return lists

        def load_words(name, src, queue):
            table = keep.tile([P, src.shape[2]], I32, name=name, tag=name, align_bytes=64)
            queue.dma_start(table[:], src[0].rearrange("p c r -> p (c r)").bitcast(I32))
            return table

        d_byte_table = keep.tile([P, G], U8, align_bytes=64)
        x_byte_table = keep.tile([P, T], U8, align_bytes=64)
        nc.vector.memset(d_byte_table[:].bitcast(I32), 0)
        nc.vector.memset(x_byte_table[:].bitcast(I32), 0)

        warm = keep.tile([P, 1], F32, tag="x_word_table", align_bytes=64)
        nc.gpsimd.memset(warm[:], 0.0)
        nc.scalar.activation(warm[:], warm[:], ACT.Sigmoid)

        d_word_table = load_words("d_word_table", d_words, nc.sync)
        k1_list = load_list("k1_list", k1)
        offs_list = load_list("offs_list", offs)
        k2_list = load_list("k2_list", k2)
        n1_list = load_list("n1_list", n1)
        n3_list = load_list("n3_list", n3)
        n4_list = load_list("n4_list", n4)
        n2_list = load_list("n2_list", n2)
        gain = keep.tile([P, PACK], F32)
        nc.scalar.dma_start(gain[:], gs.rearrange("(p t) o -> p (t o)", t=PACK))
        nc.scalar.dma_start(d_byte_table[:].bitcast(I32)[0:P:BLOCK_PARTITIONS, :], d_scales[0].bitcast(I32))
        for q in range(P // QUADRANT):
            nc.scalar.dma_start(
                x_byte_table[:].bitcast(I32)[QUADRANT * q : QUADRANT * q + PACK, :],
                x_scales[0].bitcast(I32)[PACK * q : PACK * (q + 1), :],
            )
        x_word_table = load_words("x_word_table", x_words, nc.scalar)

        def pick(name, table, dtype, lists, tag):
            picked = keep.tile([P, H], dtype, name=name, tag=tag, align_bytes=64)
            nc.vector.tensor_copy(picked[:], table.indirect(lists[:]))
            return picked

        def deal_tiles(dealt, picked, run, tiles):
            nc.vector.tensor_copy(
                dealt[:].rearrange("p (t c i) -> p c t i", t=PACK, i=run)[:, :, tiles, :],
                picked[:].rearrange("p (c i t) -> p c t i", t=PACK, i=run)[:, :, tiles, :],
            )

        def deal(name, picked, dtype, run):
            dealt = keep.tile([P, H], dtype, name=name, align_bytes=64)
            deal_tiles(dealt, picked, run, slice(0, PACK))
            return dealt

        def place(name, dealt):
            placed = keep.tile([P, H], U8, name=name, align_bytes=64)
            nc.gpsimd.memset(placed[:].bitcast(I32), 0)
            for q in range(P // QUADRANT):
                nc.sync.dma_start(
                    placed[:].bitcast(I32)[QUADRANT * q : QUADRANT * q + PACK, :],
                    dealt[:].bitcast(I32)[QUADRANT * q : QUADRANT * (q + 1) : BLOCK_PARTITIONS, :],
                )
            return placed

        def multiply(out, w_words, w_scales, t, rhs_words, rhs_scales):
            features = slice(t * P, (t + 1) * P)
            nc.tensor.matmul_mx(
                out=out,
                lhsT=w_words[:, features].bitcast(FP8X4),
                lhsT_scale=w_scales[:, features],
                rhs=rhs_words.bitcast(FP8X4),
                rhs_scale=rhs_scales,
                start=True,
                stop=True,
            )

        def quantise(codes, scales, woven, cols):
            nc.vector.quantize_mx(
                out=codes[:, cols].bitcast(FP8X4),
                scales=scales[:, cols],
                in_=woven[:, PACK * cols.start : PACK * cols.stop],
            )

        word_run, byte_run = LINE // 4, LINE
        w1_words_picked = pick("w1_words_picked", d_word_table[:].bitcast(U32), U32, k1_list, "w1_words_picked")
        w1_bytes_picked = pick("w1_bytes_picked", d_byte_table[:], U8, k1_list, "w1_bytes_picked")
        w1_words = deal("w1_words", w1_words_picked, U32, word_run)
        w1_scales = place("w1_scales", deal("w1_bytes", w1_bytes_picked, U8, byte_run))

        token_banks = [slice(u * BANK, (u + 1) * BANK) for u in range(S // BANK)]
        x_bytes = [keep.tile([P, BANK], U8, name="x_bytes%d" % u, align_bytes=64) for u in range(S // BANK)]
        x_codes = [keep.tile([P, BANK], U32, name="x_codes%d" % u, align_bytes=64) for u in range(S // BANK)]
        for u, tokens in enumerate(token_banks):
            nc.vector.tensor_copy(x_bytes[u][:], x_byte_table[:].indirect(entries(offs_list, tokens)))
        for u, tokens in enumerate(token_banks):
            nc.vector.tensor_copy(x_codes[u][:], x_word_table[:].bitcast(U32).indirect(entries(offs_list, tokens)))

        h = [keep.tile([P, S], F32, name="h%d" % t) for t in range(PACK)]
        order = [(t, u) for u in range(S // BANK) for t in (0, 1)] + [(t, u) for t in (2, 3) for u in range(S // BANK)]
        for t, u in order:
            acc = psum.tile([P, BANK], F32, name="acc")
            multiply(acc[:], w1_words, w1_scales, t, x_codes[u][:], x_bytes[u][:])
            nc.scalar.activation(h[t][:, token_banks[u]], acc[:], ACT.Copy, scale=SIXTEENTH)

        w2_bytes_picked = pick("w2_bytes_picked", d_byte_table[:], U8, k2_list, "x_word_table")
        w2_scales = place("w2_scales", deal("w2_bytes", w2_bytes_picked, U8, byte_run))

        z_woven = keep.tile([P, V * PACK], BF16, align_bytes=64)
        for c, cols in enumerate(HALVES):
            n = cols.stop - cols.start
            larger = keep.tile([P, PACK, n], F32, name="larger%d" % c)
            z_rows = keep.tile([P, PACK, n], BF16, name="z_rows%d" % c, tag="z_rows%d" % c, align_bytes=64)
            for two in range(PACK // 2):
                lined = keep.tile([P, 2, 2 * n], F32, name="lined%d_%d" % (c, two), tag="lined%d" % ((c + two) % 2))
                for e in range(2):
                    neighbours = entries(n1_list, slice(2 * cols.start, 2 * cols.stop))
                    nc.vector.tensor_copy(lined[:, e, :], h[2 * two + e][:].indirect(neighbours))
                pairs = lined[:].rearrange("p t (v n) -> p t v n", n=2)
                for e in range(2):
                    nc.vector.tensor_tensor(larger[:, 2 * two + e, :], pairs[:, e, :, 0], pairs[:, e, :, 1], ALU.max)
            for t in range(PACK):
                nc.scalar.activation(z_rows[:, t, :], larger[:, t, :], ACT.Copy, scale=gain[:, t : t + 1])
            weave(nc.scalar.copy, z_woven[:, PACK * cols.start : PACK * cols.stop], z_rows, slice(0, n))

        z_codes = keep.tile([P, V], U32, align_bytes=64)
        z_bytes = keep.tile([P, V], U8, align_bytes=64)
        w2_words_picked = pick("w2_words_picked", d_word_table[:].bitcast(U32), U32, k2_list, "z_rows0")
        quantise(z_codes, z_bytes, z_woven, HALVES[0])
        w2_words = keep.tile([P, H], U32, align_bytes=64)
        deal_tiles(w2_words, w2_words_picked, word_run, slice(0, 1))
        quantise(z_codes, z_bytes, z_woven, HALVES[1])

        h2 = [keep.tile([P, 2 * V], F32, name="h2_%d" % t) for t in range(PACK)]
        for t in range(PACK):
            nc.gpsimd.memset(h2[t][:, V:], 0.0)

        def second_layer(t, cols, copy_out):
            acc = psum.tile([P, BANK], F32, name="acc")
            multiply(acc[:, cols], w2_words, w2_scales, t, z_codes[:, cols], z_bytes[:, cols])
            copy_out(h2[t][:, cols], acc[:, cols], SIXTEENTH)

        gate, rest, far, near, mixed = (
            keep.tile([P, PACK, V], F32, name=name) for name in ("gate", "rest", "far", "near", "mixed")
        )
        out_woven = keep.tile([P, V * PACK], BF16, align_bytes=64)
        out_codes = keep.tile([P, V], U32, align_bytes=64)
        out_bytes = keep.tile([P, V], U8, align_bytes=64)
        out_rows = out_0.rearrange("(p t) v -> p t v", t=PACK)
        out_words = out_1[0].rearrange("p c r -> p (c r)").bitcast(I32)

        def fetch_gate(t, cols):
            nc.scalar.activation(gate[:, t, cols], h2[t][:].indirect(entries(n3_list, cols)), ACT.Sigmoid)

        def fetch_weights(t, cols):
            fetch_gate(t, cols)
            nc.scalar.activation(rest[:, t, cols], gate[:, t, cols], ACT.Copy, scale=-1.0, bias=1.0)

        def fetch_terms(t, cols):
            nc.vector.tensor_tensor(
                far[:, t, cols], h2[t][:].indirect(entries(n4_list, cols)), gate[:, t, cols], ALU.mult
            )
            nc.vector.tensor_tensor(
                near[:, t, cols], h2[t][:].indirect(entries(n2_list, cols)), rest[:, t, cols], ALU.mult
            )

        def fetch_terms_before_gate(t):
            step = keep.tile([P, V], F32)
            for cols in HALVES:
                nc.vector.tensor_copy(near[:, t, cols], h2[t][:].indirect(entries(n2_list, cols)))
            for cols in HALVES:
                nc.vector.tensor_tensor(
                    step[:, cols], h2[t][:].indirect(entries(n4_list, cols)), near[:, t, cols], ALU.subtract
                )
            for cols in HALVES:
                nc.vector.tensor_tensor(far[:, t, cols], step[:, cols], gate[:, t, cols], ALU.mult)

        def add(t, cols):
            nc.vector.tensor_tensor(mixed[:, t, cols], near[:, t, cols], far[:, t, cols], ALU.add)

        def store(t, cols):
            nc.sync.dma_start(out_rows[:, t, cols], mixed[:, t, cols])

        def hand_on(cols):
            quantise(out_codes, out_bytes, out_woven, cols)
            nc.sync.dma_start(out_words[:, cols], out_codes[:, cols].bitcast(I32))

        second_layer(0, HALVES[0], nc.scalar.mul)
        deal_tiles(w2_words, w2_words_picked, word_run, slice(1, PACK))
        second_layer(0, HALVES[1], nc.vector.tensor_scalar_mul)
        fetch_gate(0, WHOLE)
        second_layer(1, WHOLE, nc.scalar.mul)
        fetch_terms_before_gate(0)
        last = PACK - 1
        for t in range(1, last):
            fetch_weights(t, WHOLE)
            second_layer(t + 1, WHOLE, nc.scalar.mul)
            fetch_terms(t, WHOLE)
            add(t - 1, WHOLE)
            store(t - 1, WHOLE)
        add(last - 1, WHOLE)
        store(last - 1, WHOLE)
        for cols in HALVES:
            fetch_weights(last, cols)
        fetch_terms(last, HALVES[0])
        add(last, HALVES[0])
        store(last, HALVES[0])
        fetch_terms(last, HALVES[1])
        weave(nc.scalar.copy, out_woven, mixed, HALVES[0])
        for cols in LAST_QUARTERS:
            add(last, cols)
        store(last, HALVES[1])
        weave(nc.scalar.copy, out_woven, mixed, LAST_QUARTERS[0])
        hand_on(HALVES[0])
        weave(nc.vector.tensor_copy, out_woven, mixed, LAST_QUARTERS[1])
        hand_on(HALVES[1])
        for q in range(P // QUADRANT):
            queue = nc.scalar if q % 2 else nc.sync
            queue.dma_start(
                out_2[0].bitcast(I32)[PACK * q : PACK * (q + 1), :],
                out_bytes[:].bitcast(I32)[QUADRANT * q : QUADRANT * q + PACK, :],
            )
